import numpy as np
import ml_dtypes


def mxq(x, axis, fmt="e4m3"):
    dtype, down = {"e4m3": (ml_dtypes.float8_e4m3fn, 7), "e5m2": (ml_dtypes.float8_e5m2, 14)}[fmt]
    v = np.moveaxis(np.asarray(x, np.float32).astype(ml_dtypes.bfloat16).astype(np.float64), axis, -1)
    blocks = v.reshape(v.shape[:-1] + (-1, 32))
    amax = np.abs(blocks).max(-1, keepdims=True)
    byte = np.maximum(np.where(amax > 0, np.frexp(amax)[1] - 1 + 127, 0) - down, 1)
    scale = np.exp2(byte - 127.0)
    codes = (blocks / scale).astype(np.float32).astype(dtype).astype(np.float64)
    return np.moveaxis((codes * scale).reshape(v.shape), -1, axis)


WIDE = False


def mx_kscale(k):
    if not WIDE:
        return np.ones(k)
    levels = np.array([10, -10, 5, -5, 0])
    if k % 512:
        return np.exp2(np.random.permutation(np.resize(levels, k // 32))).repeat(32)
    a = np.empty((k // 512, 16))
    for p in range(k // 512):
        a[p, :8] = np.random.permutation(np.resize(levels, 8))
        for g in range(8):
            far = levels[np.abs(levels - a[p, g]) >= 10]
            a[p, g + 8] = far[np.random.randint(len(far))]
    return np.exp2(a.ravel()).repeat(32)


def f64(x):
    return np.asarray(x).astype(np.float64)


def striped(idx):
    return np.tile(idx.reshape(-1, 16).T, (8, 1)).astype(np.uint16)


def unstriped(offs):
    return offs[:16].T.reshape(-1).astype(np.int64)


def pack_weight(w):
    k, n = w.shape
    w = f64(np.asarray(w, np.float32).astype(ml_dtypes.bfloat16)).reshape(k // 32, 32, n)
    amax = np.abs(w).max(1)
    byte = np.clip(np.where(amax > 0, np.frexp(amax)[1] - 1 + 127 - 7, 1), 1, 254)
    scaled = (w * np.exp2(127.0 - byte)[:, None, :]).reshape(k, n).astype(np.float32)
    words = np.ascontiguousarray(scaled.reshape(k // 512, 128, 4, n).transpose(0, 1, 3, 2)).astype(ml_dtypes.float8_e4m3fn).view(np.uint8)
    return words, np.ascontiguousarray(byte.astype(np.uint8).reshape(k // 512, 16, n))


def unpack_weight(words, scales):
    g, p, n, _ = words.shape
    vals = np.ascontiguousarray(words).view(ml_dtypes.float8_e4m3fn).astype(np.float64) * np.repeat(np.exp2(scales.astype(np.float64) - 127.0), 8, axis=1)[..., None]
    return vals.transpose(0, 1, 3, 2).reshape(g * 512, n)


def gelu(v):
    return 0.5 * v * (1.0 + np.tanh(np.sqrt(2.0 / np.pi) * (v + 0.044715 * v**3)))


K, T, S, H, N = 512, 2048, 1024, 512, 128
P = 2 ** 7


def setup_inputs():
    n = np.random.standard_normal
    s = mx_kscale(K)[:, None]
    u = mx_kscale(H)
    packed_xT = pack_weight(n((K, T)) * s)
    packed_w2 = pack_weight(n((H, N)) / np.sqrt(H) / u[:, None])
    return {
        "x_words": packed_xT[0],
        "x_scales": packed_xT[1],
        "w1": (n((K, H)) / np.sqrt(K) / s * u).astype(np.float32),
        "w2_words": packed_w2[0],
        "w2_scales": packed_w2[1],
        "lam": np.tile(np.random.uniform(0.1, 0.9, S), (P, 1)).astype(np.float32),
        "mu": np.tile(np.random.uniform(0.1, 0.9, S), (P, 1)).astype(np.float32),
        "offs": striped(np.random.permutation(T)[:S]),
        "pos1": striped(np.random.permutation(S)),
    }


def reference(x_words, x_scales, w1, w2_words, w2_scales, lam, mu, offs, pos1):
    xq = unpack_weight(x_words, x_scales)[:, unstriped(offs)]
    h = gelu(mxq(f64(w1), 0, "e4m3").T @ xq)
    z = h * f64(lam)[:1] + h[:, unstriped(pos1)] * f64(mu)[:1]
    return unpack_weight(w2_words, w2_scales).T @ mxq(z, 0, "e4m3")

@@ -1,0 +1,138 @@
+from contextlib import ExitStack
+
+import concourse.mybir as mybir
+from concourse.masks import make_identity
+
+K, T, S, H, N = 512, 2048, 1024, 512, 128
+FLOPS = 2 * K * H * S + 2 * H * N * S
+
+F32 = mybir.dt.float32
+BF16 = mybir.dt.bfloat16
+I32 = mybir.dt.int32
+U32 = mybir.dt.uint32
+U16 = mybir.dt.uint16
+U8 = mybir.dt.uint8
+FP8X4 = mybir.dt.float8_e4m3fn_x4
+ACT = mybir.ActivationFunctionType
+ALU = mybir.AluOpType
+
+P = 128
+PACK = 4
+HALF = 512
+LIST_ROWS = 16
+FINE = ((0, 512), (512, 256), (768, 256))
+COARSE = ((0, 512), (512, 512))
+GROUPS = ((0, 512), (512, 256), (768, 128), (896, 128))
+
+
+def tile_picked_mixup_gelu_p_kernel(tc, x_words, x_scales, w1, w2_words, w2_scales, lam, mu, offs, pos1, out):
+    nc = tc.nc
+    with ExitStack() as ctx:
+        keep = ctx.enter_context(tc.tile_pool(name="keep", bufs=1))
+        psum = ctx.enter_context(tc.psum_pool(name="psum", bufs=1))
+
+        offs_sb = keep.tile([P, S // LIST_ROWS], U16, name="offs_sb")
+        pos_sb = keep.tile([P, S // LIST_ROWS], U16, name="pos_sb")
+        xs_all = keep.tile([P, T], U8, name="xs_all", align_bytes=64)
+        xw_all = keep.tile([P, T], I32, name="xw_all", align_bytes=64)
+        w1_raw = [keep.tile([P, PACK, H // 2], F32, name=f"w1_raw{a}", align_bytes=64) for a in range(2)]
+        mu_sb = keep.tile([P, S], F32, name="mu_sb", align_bytes=64)
+        lam_col = keep.tile([P, S // P], F32, name="lam_col", align_bytes=64)
+        w2w = keep.tile([P, N], I32, name="w2w", align_bytes=64)
+        w2s = keep.tile([P, N], U8, name="w2s", align_bytes=64)
+        ident = keep.tile([P, P], F32, name="ident", align_bytes=64)
+
+        nc.vector.memset(xs_all[:].bitcast(I32), 0)
+        w1_rows = w1.rearrange("(p j) c -> p j c", j=PACK)
+        nc.sync.dma_start(w1_raw[0][:], w1_rows[:, :, : H // 2])
+        nc.sync.dma_start(offs_sb[:], offs)
+        for q in range(4):
+            nc.sync.dma_start(xs_all[32 * q : 32 * q + 4, :].bitcast(I32), x_scales[0, 4 * q : 4 * q + 4, :].bitcast(I32))
+        nc.sync.dma_start(w1_raw[1][:], w1_rows[:, :, H // 2 :])
+        nc.sync.dma_start(xw_all[:], x_words[0].rearrange("p c r -> p (c r)").bitcast(I32))
+        nc.sync.dma_start(pos_sb[:], pos1)
+        nc.sync.dma_start(mu_sb[:], mu)
+        with nc.allow_non_contiguous_dma(reason="one share a partition"):
+            nc.sync.dma_start(lam_col[:], lam[0].rearrange("(c p) -> p c", p=P))
+        nc.sync.dma_start(w2w[:], w2_words[0].rearrange("p c r -> p (c r)").bitcast(I32))
+        nc.gpsimd.memset(w2s[:].bitcast(I32), 0)
+        for q in range(4):
+            nc.sync.dma_start(w2s[32 * q : 32 * q + 4, :].bitcast(I32), w2_scales[0, 4 * q : 4 * q + 4, :].bitcast(I32))
+        make_identity(nc, ident[:])
+
+        def entries(lst, j0, n):
+            return lst[:, j0 // LIST_ROWS : (j0 + n) // LIST_ROWS]
+
+        xs = keep.tile([P, S], U8, name="xs", align_bytes=64)
+        xw = keep.tile([P, S], U32, name="xw", align_bytes=64)
+        nc.vector.tensor_copy(xs[:], xs_all[:].indirect(offs_sb[:]))
+
+        w1_bf = keep.tile([P, PACK, P, PACK], BF16, name="w1_bf", align_bytes=64)
+        dst = w1_bf[:].rearrange("p t m j -> p m j t")
+        for a in range(2):
+            nc.scalar.copy(dst[:, 64 * a : 64 * (a + 1)], w1_raw[a][:].rearrange("p j (m t) -> p m j t", t=PACK))
+        w1w = keep.tile([P, H], U32, name="w1w", align_bytes=64)
+        w1s = keep.tile([P, H], U8, name="w1s", align_bytes=64)
+        nc.vector.quantize_mx(out=w1w[:].bitcast(FP8X4), scales=w1s[:], in_=w1_bf[:].rearrange("p t m j -> p (t m j)"))
+
+        for j0, n in FINE:
+            nc.vector.tensor_copy(xw[:, j0 : j0 + n], xw_all[:].bitcast(U32).indirect(entries(offs_sb, j0, n)))
+
+        h = [keep.tile([P, S], F32, name=f"h{t}", align_bytes=64) for t in range(PACK)]
+        for t in range(PACK):
+            cols = slice(t * P, (t + 1) * P)
+            for j0, n in FINE if t == 0 else COARSE:
+                u = psum.tile([P, HALF], F32, name="u", tag="acc", bufs=2)
+                nc.tensor.matmul_mx(out=u[:, :n], lhsT=w1w[:, cols].bitcast(FP8X4), lhsT_scale=w1s[:, cols],
+                                    rhs=xw[:, j0 : j0 + n].bitcast(FP8X4), rhs_scale=xs[:, j0 : j0 + n], start=True, stop=True)
+                nc.scalar.activation(h[t][:, j0 : j0 + n], u[:, :n], ACT.Gelu_apprx_tanh)
+
+        partner = [keep.tile([P, PACK, HALF], F32, name=f"partner{a}", align_bytes=64) for a in range(2)]
+        for t in range(PACK):
+            for a in range(2):
+                nc.vector.tensor_tensor(partner[a][:, t, :], h[t][:].indirect(entries(pos_sb, a * HALF, HALF)),
+                                        mu_sb[:, a * HALF : (a + 1) * HALF], ALU.mult)
+
+        own = [keep.tile([P, PACK, P], F32, name=f"own{c}", align_bytes=64) for c in range(S // P)]
+        for c in range(S // P):
+            turned = psum.tile([P, PACK, P], F32, name="turned", tag="turned", bufs=3)
+            for t in range(PACK):
+                nc.tensor.transpose(turned[:, t, :], h[t][:, c * P : (c + 1) * P], ident[:])
+            nc.scalar.activation(own[c][:], turned[:], ACT.Copy, scale=lam_col[:, c : c + 1])
+
+        z_bf = [keep.tile([P, n, PACK], BF16, name=f"z_bf{j0}", align_bytes=64) for j0, n in GROUPS]
+
+        def mix(c):
+            back = psum.tile([P, PACK, P], F32, name="back", tag="back", bufs=3)
+            for t in range(PACK):
+                nc.tensor.transpose(back[:, t, :], own[c][:, t, :], ident[:])
+            g = max(i for i, (j0, n) in enumerate(GROUPS) if j0 <= c * P)
+            lo = c * P - GROUPS[g][0]
+            a, lo_a = divmod(c * P, HALF)
+            nc.vector.tensor_tensor(
+                z_bf[g][:, lo : lo + P, :].rearrange("p (c i) t -> p c t i", i=4),
+                back[:].rearrange("p t (c i) -> p c t i", i=4),
+                partner[a][:, :, lo_a : lo_a + P].rearrange("p t (c i) -> p c t i", i=4),
+                ALU.add,
+            )
+
+        def finish(g):
+            j0, n = GROUPS[g]
+            zw = keep.tile([P, n], U32, name=f"zw{g}", align_bytes=64)
+            zs = keep.tile([P, n], U8, name=f"zs{g}", align_bytes=64)
+            nc.vector.quantize_mx(out=zw[:].bitcast(FP8X4), scales=zs[:], in_=z_bf[g][:].rearrange("p n t -> p (n t)"))
+            y = psum.tile([P, HALF], F32, name="y", tag="acc", bufs=2)
+            nc.tensor.matmul_mx(out=y[:, :n], lhsT=w2w[:].bitcast(FP8X4), lhsT_scale=w2s[:],
+                                rhs=zw[:].bitcast(FP8X4), rhs_scale=zs[:], start=True, stop=True)
+            y_sb = keep.tile([P, n], F32, name=f"y_sb{g}", align_bytes=64)
+            nc.scalar.copy(y_sb[:], y[:, :n])
+            nc.sync.dma_start(out[:, j0 : j0 + n], y_sb[:])
+
+        done = 0
+        for c in range(S // P):
+            mix(c)
+            while done < len(GROUPS) and sum(GROUPS[done]) <= c * P:
+                finish(done)
+                done += 1
+        for g in range(done, len(GROUPS)):
+            finish(g)

@@ -22,7 +22,12 @@ HALF = 512
 LIST_ROWS = 16
 FINE = ((0, 512), (512, 256), (768, 256))
 COARSE = ((0, 512), (512, 512))
-GROUPS = ((0, 512), (512, 256), (768, 128), (896, 128))
+GROUP = 256
+TURNED = 6
+W1_PARTS = ((0, 320), (320, 192))
+RUN = S // P
+REL_FLOOR = 2.0**-40
+ABS_FLOOR = 2.0**-100
 
 
 def tile_picked_mixup_gelu_p_kernel(tc, x_words, x_scales, w1, w2_words, w2_scales, lam, mu, offs, pos1, out):
@@ -31,37 +36,61 @@ def tile_picked_mixup_gelu_p_kernel(tc, x_words, x_scales, w1, w2_words, w2_scal
         keep = ctx.enter_context(tc.tile_pool(name="keep", bufs=1))
         psum = ctx.enter_context(tc.psum_pool(name="psum", bufs=1))
 
+        banks = [psum.tile([P, HALF], F32, name=f"bank{b}") for b in range(8)]
+
+        def quarters(b):
+            return banks[b][:].rearrange("p (t n) -> p t n", t=PACK)
+
         offs_sb = keep.tile([P, S // LIST_ROWS], U16, name="offs_sb")
         pos_sb = keep.tile([P, S // LIST_ROWS], U16, name="pos_sb")
         xs_all = keep.tile([P, T], U8, name="xs_all", align_bytes=64)
-        xw_all = keep.tile([P, T], I32, name="xw_all", align_bytes=64)
-        w1_raw = [keep.tile([P, PACK, H // 2], F32, name=f"w1_raw{a}", align_bytes=64) for a in range(2)]
-        mu_sb = keep.tile([P, S], F32, name="mu_sb", align_bytes=64)
-        lam_col = keep.tile([P, S // P], F32, name="lam_col", align_bytes=64)
+        xw_all = keep.tile([P, T], I32, name="xw_all", tag="xw_all", align_bytes=64)
+        w1_raw = [keep.tile([P, PACK, n], F32, name=f"w1_raw{c0}", align_bytes=64) for c0, n in W1_PARTS]
+        shares = keep.tile([P, 2, RUN], F32, name="shares", align_bytes=64)
+        lam_wide = keep.tile([P, GROUP], F32, name="lam_wide", align_bytes=64)
+        lam_col = keep.tile([P, TURNED], F32, name="lam_col", align_bytes=64)
         w2w = keep.tile([P, N], I32, name="w2w", align_bytes=64)
         w2s = keep.tile([P, N], U8, name="w2s", align_bytes=64)
         ident = keep.tile([P, P], F32, name="ident", align_bytes=64)
 
         nc.vector.memset(xs_all[:].bitcast(I32), 0)
         w1_rows = w1.rearrange("(p j) c -> p j c", j=PACK)
-        nc.sync.dma_start(w1_raw[0][:], w1_rows[:, :, : H // 2])
         nc.sync.dma_start(offs_sb[:], offs)
+        nc.sync.dma_start(shares[:, 0, :], lam[0].rearrange("(p e) -> p e", e=RUN))
+        nc.sync.dma_start(shares[:, 1, :], mu[0].rearrange("(p e) -> p e", e=RUN))
+        nc.sync.dma_start(w1_raw[0][:], w1_rows[:, :, : W1_PARTS[0][1]])
         for q in range(4):
             nc.sync.dma_start(xs_all[32 * q : 32 * q + 4, :].bitcast(I32), x_scales[0, 4 * q : 4 * q + 4, :].bitcast(I32))
-        nc.sync.dma_start(w1_raw[1][:], w1_rows[:, :, H // 2 :])
+        nc.sync.dma_start(w1_raw[1][:], w1_rows[:, :, W1_PARTS[1][0] :])
         nc.sync.dma_start(xw_all[:], x_words[0].rearrange("p c r -> p (c r)").bitcast(I32))
         nc.sync.dma_start(pos_sb[:], pos1)
-        nc.sync.dma_start(mu_sb[:], mu)
-        with nc.allow_non_contiguous_dma(reason="one share a partition"):
-            nc.sync.dma_start(lam_col[:], lam[0].rearrange("(c p) -> p c", p=P))
-        nc.sync.dma_start(w2w[:], w2_words[0].rearrange("p c r -> p (c r)").bitcast(I32))
-        nc.gpsimd.memset(w2s[:].bitcast(I32), 0)
-        for q in range(4):
-            nc.sync.dma_start(w2s[32 * q : 32 * q + 4, :].bitcast(I32), w2_scales[0, 4 * q : 4 * q + 4, :].bitcast(I32))
         make_identity(nc, ident[:])
 
         def entries(lst, j0, n):
             return lst[:, j0 // LIST_ROWS : (j0 + n) // LIST_ROWS]
+
+        def small(name, *shape):
+            return keep.tile([P, *shape], F32, name=name, align_bytes=64)
+
+        sizes = small("sizes", 2, RUN)
+        sign2, floor, size, lam_safe, inverse, factor = (small(n, RUN) for n in ("sign2", "floor", "size", "lam_safe", "inverse", "factor"))
+        split = TURNED * P // RUN
+        nc.vector.scalar_tensor_tensor(sizes[:], shares[:], -1.0, shares[:], ALU.mult, ALU.max)
+        nc.vector.tensor_scalar(sign2[:], shares[:, 0, :], 0.0, 2.0, ALU.is_ge, ALU.mult)
+        nc.vector.tensor_scalar(floor[:], sizes[:, 1, :], REL_FLOOR, ABS_FLOOR, ALU.mult, ALU.add)
+        nc.vector.tensor_copy(factor[split:, :], shares[split:, 1, :])
+        nc.vector.tensor_tensor(size[:], floor[:], sizes[:, 0, :], ALU.max)
+        nc.vector.scalar_tensor_tensor(lam_safe[:], sign2[:], -1.0, size[:], ALU.add, ALU.mult)
+        nc.vector.reciprocal(inverse[:], lam_safe[:])
+        nc.vector.tensor_tensor(factor[:split, :], shares[:split, 1, :], inverse[:split, :], ALU.mult)
+        nc.sync.dma_start(out[0].rearrange("(p e) -> p e", e=RUN), lam_safe[:])
+        nc.sync.dma_start(w2w[:], w2_words[0].rearrange("p c r -> p (c r)").bitcast(I32))
+        nc.gpsimd.memset(w2s[:].bitcast(I32), 0)
+        for q in range(4):
+            nc.sync.dma_start(w2s[32 * q : 32 * q + 4, :].bitcast(I32), w2_scales[0, 4 * q : 4 * q + 4, :].bitcast(I32))
+        nc.sync.dma_start(lam_wide[:], lam[:, TURNED * P :])
+        with nc.allow_non_contiguous_dma(reason="one share a partition"):
+            nc.sync.dma_start(lam_col[:], out[0, : TURNED * P].rearrange("(c p) -> p c", p=P))
 
         xs = keep.tile([P, S], U8, name="xs", align_bytes=64)
         xw = keep.tile([P, S], U32, name="xw", align_bytes=64)
@@ -69,70 +98,108 @@ def tile_picked_mixup_gelu_p_kernel(tc, x_words, x_scales, w1, w2_words, w2_scal
 
         w1_bf = keep.tile([P, PACK, P, PACK], BF16, name="w1_bf", align_bytes=64)
         dst = w1_bf[:].rearrange("p t m j -> p m j t")
-        for a in range(2):
-            nc.scalar.copy(dst[:, 64 * a : 64 * (a + 1)], w1_raw[a][:].rearrange("p j (m t) -> p m j t", t=PACK))
-        w1w = keep.tile([P, H], U32, name="w1w", align_bytes=64)
+        for raw, (c0, n) in zip(w1_raw, W1_PARTS):
+            nc.scalar.copy(dst[:, c0 // PACK : (c0 + n) // PACK], raw[:].rearrange("p j (m t) -> p m j t", t=PACK))
+        factors = keep.tile([P, S], F32, name="factors", align_bytes=64)
+        for e0 in range(0, RUN, PACK):
+            spread = quarters(3 + e0 // PACK)
+            for i in range(PACK):
+                nc.tensor.transpose(spread[:, i, :], factor[:, e0 + i : e0 + i + 1].to_broadcast([P, P]), ident[:])
+            nc.scalar.copy(factors[:].rearrange("q (n e) -> q n e", e=RUN)[:, :, e0 : e0 + PACK], spread.rearrange("q e n -> q n e"))
         w1s = keep.tile([P, H], U8, name="w1s", align_bytes=64)
-        nc.vector.quantize_mx(out=w1w[:].bitcast(FP8X4), scales=w1s[:], in_=w1_bf[:].rearrange("p t m j -> p (t m j)"))
+        w1w_first = keep.tile([P, P], U32, name="w1w_first", align_bytes=64)
+        nc.vector.quantize_mx(out=w1w_first[:].bitcast(FP8X4), scales=w1s[:, :P], in_=w1_bf[:, 0].rearrange("p m j -> p (m j)"))
 
         for j0, n in FINE:
             nc.vector.tensor_copy(xw[:, j0 : j0 + n], xw_all[:].bitcast(U32).indirect(entries(offs_sb, j0, n)))
 
-        h = [keep.tile([P, S], F32, name=f"h{t}", align_bytes=64) for t in range(PACK)]
+        w1w_rest = keep.tile([P, H - P], U32, name="w1w_rest", tag="xw_all", align_bytes=64)
+        nc.vector.quantize_mx(out=w1w_rest[:, :P].bitcast(FP8X4), scales=w1s[:, P : 2 * P], in_=w1_bf[:, 1].rearrange("p m j -> p (m j)"))
+        nc.vector.quantize_mx(out=w1w_rest[:, P:].bitcast(FP8X4), scales=w1s[:, 2 * P :], in_=w1_bf[:, 2:].rearrange("p t m j -> p (t m j)"))
+        w1w = [w1w_first[:]] + [w1w_rest[:, i * P : (i + 1) * P] for i in range(PACK - 1)]
+
+        h = [keep.tile([P, S], F32, name=f"h{t}", tag=f"h{t}", align_bytes=64) for t in range(PACK)]
+        made = 0
         for t in range(PACK):
             cols = slice(t * P, (t + 1) * P)
             for j0, n in FINE if t == 0 else COARSE:
-                u = psum.tile([P, HALF], F32, name="u", tag="acc", bufs=2)
-                nc.tensor.matmul_mx(out=u[:, :n], lhsT=w1w[:, cols].bitcast(FP8X4), lhsT_scale=w1s[:, cols],
+                u = banks[made % 3]
+                made += 1
+                nc.tensor.matmul_mx(out=u[:, :n], lhsT=w1w[t].bitcast(FP8X4), lhsT_scale=w1s[:, cols],
                                     rhs=xw[:, j0 : j0 + n].bitcast(FP8X4), rhs_scale=xs[:, j0 : j0 + n], start=True, stop=True)
                 nc.scalar.activation(h[t][:, j0 : j0 + n], u[:, :n], ACT.Gelu_apprx_tanh)
 
-        partner = [keep.tile([P, PACK, HALF], F32, name=f"partner{a}", align_bytes=64) for a in range(2)]
-        for t in range(PACK):
-            for a in range(2):
-                nc.vector.tensor_tensor(partner[a][:, t, :], h[t][:].indirect(entries(pos_sb, a * HALF, HALF)),
-                                        mu_sb[:, a * HALF : (a + 1) * HALF], ALU.mult)
+        partner = {}
+        total = [quarters(b) for b in (3, 4, 5, 6, 7, 3)]
+        back_bank = (0, 1, 2, 0, 1, 2)
+        y_bank = {0: 4, 256: 5, 512: 6, 768: 7, 896: 3}
 
-        own = [keep.tile([P, PACK, P], F32, name=f"own{c}", align_bytes=64) for c in range(S // P)]
-        for c in range(S // P):
-            turned = psum.tile([P, PACK, P], F32, name="turned", tag="turned", bufs=3)
-            for t in range(PACK):
-                nc.tensor.transpose(turned[:, t, :], h[t][:, c * P : (c + 1) * P], ident[:])
-            nc.scalar.activation(own[c][:], turned[:], ACT.Copy, scale=lam_col[:, c : c + 1])
+        def fetch(g, t):
+            j0 = g * GROUP
+            if t == 0:
+                partner[g] = keep.tile([P, PACK, GROUP], F32, name="partner", tag="partner", bufs=2, align_bytes=64)
+            nc.vector.tensor_tensor(partner[g][:, t, :], h[t][:].indirect(entries(pos_sb, j0, GROUP)), factors[:, j0 : j0 + GROUP], ALU.mult)
 
-        z_bf = [keep.tile([P, n, PACK], BF16, name=f"z_bf{j0}", align_bytes=64) for j0, n in GROUPS]
+        def add_turned(g, t):
+            for lo in range(0, GROUP, P):
+                c = (g * GROUP + lo) // P
+                nc.tensor.matmul(total[c][:, t, :], h[t][:, c * P : (c + 1) * P], ident[:], start=(t == 0), stop=False, is_transpose=True)
+                nc.tensor.matmul(total[c][:, t, :], partner[g][:, t, lo : lo + P], ident[:], start=False, stop=(t == PACK - 1), is_transpose=True)
 
-        def mix(c):
-            back = psum.tile([P, PACK, P], F32, name="back", tag="back", bufs=3)
-            for t in range(PACK):
-                nc.tensor.transpose(back[:, t, :], own[c][:, t, :], ident[:])
-            g = max(i for i, (j0, n) in enumerate(GROUPS) if j0 <= c * P)
-            lo = c * P - GROUPS[g][0]
-            a, lo_a = divmod(c * P, HALF)
-            nc.vector.tensor_tensor(
-                z_bf[g][:, lo : lo + P, :].rearrange("p (c i) t -> p c t i", i=4),
-                back[:].rearrange("p t (c i) -> p c t i", i=4),
-                partner[a][:, :, lo_a : lo_a + P].rearrange("p t (c i) -> p c t i", i=4),
-                ALU.add,
-            )
-
-        def finish(g):
-            j0, n = GROUPS[g]
-            zw = keep.tile([P, n], U32, name=f"zw{g}", align_bytes=64)
-            zs = keep.tile([P, n], U8, name=f"zs{g}", align_bytes=64)
-            nc.vector.quantize_mx(out=zw[:].bitcast(FP8X4), scales=zs[:], in_=z_bf[g][:].rearrange("p n t -> p (n t)"))
-            y = psum.tile([P, HALF], F32, name="y", tag="acc", bufs=2)
-            nc.tensor.matmul_mx(out=y[:, :n], lhsT=w2w[:].bitcast(FP8X4), lhsT_scale=w2s[:],
-                                rhs=zw[:].bitcast(FP8X4), rhs_scale=zs[:], start=True, stop=True)
-            y_sb = keep.tile([P, n], F32, name=f"y_sb{g}", align_bytes=64)
-            nc.scalar.copy(y_sb[:], y[:, :n])
+        def second_layer(j0, n, z_bf, zw, last):
+            zs = keep.tile([P, n], U8, name=f"zs{j0}", align_bytes=64)
+            nc.vector.quantize_mx(out=zw.bitcast(FP8X4), scales=zs[:], in_=z_bf[:].rearrange("p n t -> p (n t)"))
+            y = banks[y_bank[j0]][:, :n]
+            nc.tensor.matmul_mx(out=y, lhsT=w2w[:].bitcast(FP8X4), lhsT_scale=w2s[:],
+                                rhs=zw.bitcast(FP8X4), rhs_scale=zs[:], start=True, stop=True)
+            y_sb = keep.tile([P, n], F32, name=f"y_sb{j0}", align_bytes=64)
+            if last:
+                nc.vector.tensor_copy(y_sb[:], y)
+            else:
+                nc.scalar.copy(y_sb[:], y)
             nc.sync.dma_start(out[:, j0 : j0 + n], y_sb[:])
 
-        done = 0
-        for c in range(S // P):
-            mix(c)
-            while done < len(GROUPS) and sum(GROUPS[done]) <= c * P:
-                finish(done)
-                done += 1
-        for g in range(done, len(GROUPS)):
-            finish(g)
+        def finish_turned(g):
+            j0 = g * GROUP
+            z_bf = keep.tile([P, GROUP, PACK], BF16, name=f"z_bf{j0}", tag=f"z_bf{j0}", align_bytes=64)
+            for lo in range(0, GROUP, P):
+                c = (j0 + lo) // P
+                z_t = keep.tile([P, 2, P, 2], BF16, name=f"z_t{c}", tag=f"z_t{c}", align_bytes=64)
+                nc.scalar.activation(z_t[:], total[c].rearrange("j (u e) p -> j u p e", e=2), ACT.Copy, scale=lam_col[:, c : c + 1])
+                pairs = z_t[:].rearrange("j u p e -> j (u p e)").bitcast(F32)
+                back = quarters(back_bank[c])[:, :2, :]
+                for u in range(2):
+                    nc.tensor.transpose(back[:, u, :], pairs[:, u * P : (u + 1) * P], ident[:])
+                woven = z_bf[:, lo : lo + P, :].rearrange("p j t -> p (j t)").bitcast(F32).rearrange("p (j u) -> p j u", u=2)
+                nc.scalar.copy(woven, back.rearrange("p u j -> p j u"))
+            return z_bf
+
+        for t in range(PACK):
+            for g in range(2):
+                fetch(g, t)
+                add_turned(g, t)
+        turned = [finish_turned(0)]
+        for t in range(PACK):
+            fetch(2, t)
+            add_turned(2, t)
+        turned.append(finish_turned(1))
+        j0 = TURNED * P
+        own = keep.tile([P, PACK, GROUP], F32, name="own", tag="z_t0", align_bytes=64)
+        for t in range(PACK):
+            nc.vector.tensor_tensor(own[:, t, :], h[t][:, j0:], lam_wide[:], ALU.mult)
+        turned.append(finish_turned(2))
+        for t in range(PACK):
+            fetch(3, t)
+        for g, tag in enumerate(("h2", "h3", "zw2")):
+            zw = keep.tile([P, GROUP], U32, name=f"zw{g}", tag=tag, align_bytes=64)
+            second_layer(g * GROUP, GROUP, turned[g], zw[:], False)
+        zw_last = keep.tile([P, GROUP], U32, name="zw_last", tag="z_bf512", align_bytes=64)
+        for lo in range(0, GROUP, P):
+            z_bf = keep.tile([P, P, PACK], BF16, name=f"z_bf{j0 + lo}", align_bytes=64)
+            nc.vector.tensor_tensor(
+                z_bf[:].rearrange("p (c i) t -> p c t i", i=4),
+                own[:, :, lo : lo + P].rearrange("p t (c i) -> p c t i", i=4),
+                partner[3][:, :, lo : lo + P].rearrange("p t (c i) -> p c t i", i=4),
+                ALU.add,
+            )
+            second_layer(j0 + lo, P, z_bf, zw_last[:, lo : lo + P], lo + P == GROUP)

from contextlib import ExitStack

import concourse.mybir as mybir
from concourse.masks import make_identity

K, T, S, H, N = 512, 2048, 1024, 512, 128
FLOPS = 2 * K * H * S + 2 * H * N * S

F32 = mybir.dt.float32
BF16 = mybir.dt.bfloat16
I32 = mybir.dt.int32
U32 = mybir.dt.uint32
U16 = mybir.dt.uint16
U8 = mybir.dt.uint8
FP8X4 = mybir.dt.float8_e4m3fn_x4
ACT = mybir.ActivationFunctionType
ALU = mybir.AluOpType

P = 128
PACK = 4
HALF = 512
LIST_ROWS = 16
FINE = ((0, 512), (512, 256), (768, 256))
COARSE = ((0, 512), (512, 512))
GROUP = 256
TURNED = 6
W1_PARTS = ((0, 320), (320, 192))
RUN = S // P
REL_FLOOR = 2.0**-40
ABS_FLOOR = 2.0**-100


def tile_picked_mixup_gelu_p_kernel(tc, x_words, x_scales, w1, w2_words, w2_scales, lam, mu, offs, pos1, out):
    nc = tc.nc
    with ExitStack() as ctx:
        keep = ctx.enter_context(tc.tile_pool(name="keep", bufs=1))
        psum = ctx.enter_context(tc.psum_pool(name="psum", bufs=1))

        banks = [psum.tile([P, HALF], F32, name=f"bank{b}") for b in range(8)]

        def quarters(b):
            return banks[b][:].rearrange("p (t n) -> p t n", t=PACK)

        offs_sb = keep.tile([P, S // LIST_ROWS], U16, name="offs_sb")
        pos_sb = keep.tile([P, S // LIST_ROWS], U16, name="pos_sb")
        xs_all = keep.tile([P, T], U8, name="xs_all", align_bytes=64)
        xw_all = keep.tile([P, T], I32, name="xw_all", tag="xw_all", align_bytes=64)
        w1_raw = [keep.tile([P, PACK, n], F32, name=f"w1_raw{c0}", align_bytes=64) for c0, n in W1_PARTS]
        shares = keep.tile([P, 2, RUN], F32, name="shares", align_bytes=64)
        lam_wide = keep.tile([P, GROUP], F32, name="lam_wide", align_bytes=64)
        lam_col = keep.tile([P, TURNED], F32, name="lam_col", align_bytes=64)
        w2w = keep.tile([P, N], I32, name="w2w", align_bytes=64)
        w2s = keep.tile([P, N], U8, name="w2s", align_bytes=64)
        ident = keep.tile([P, P], F32, name="ident", align_bytes=64)

        nc.vector.memset(xs_all[:].bitcast(I32), 0)
        w1_rows = w1.rearrange("(p j) c -> p j c", j=PACK)
        nc.sync.dma_start(offs_sb[:], offs)
        nc.sync.dma_start(shares[:, 0, :], lam[0].rearrange("(p e) -> p e", e=RUN))
        nc.sync.dma_start(shares[:, 1, :], mu[0].rearrange("(p e) -> p e", e=RUN))
        nc.sync.dma_start(w1_raw[0][:], w1_rows[:, :, : W1_PARTS[0][1]])
        for q in range(4):
            nc.sync.dma_start(xs_all[32 * q : 32 * q + 4, :].bitcast(I32), x_scales[0, 4 * q : 4 * q + 4, :].bitcast(I32))
        nc.sync.dma_start(w1_raw[1][:], w1_rows[:, :, W1_PARTS[1][0] :])
        nc.sync.dma_start(xw_all[:], x_words[0].rearrange("p c r -> p (c r)").bitcast(I32))
        nc.sync.dma_start(pos_sb[:], pos1)
        make_identity(nc, ident[:])

        def entries(lst, j0, n):
            return lst[:, j0 // LIST_ROWS : (j0 + n) // LIST_ROWS]

        def small(name, *shape):
            return keep.tile([P, *shape], F32, name=name, align_bytes=64)

        sizes = small("sizes", 2, RUN)
        sign2, floor, size, lam_safe, inverse, factor = (small(n, RUN) for n in ("sign2", "floor", "size", "lam_safe", "inverse", "factor"))
        split = TURNED * P // RUN
        nc.vector.scalar_tensor_tensor(sizes[:], shares[:], -1.0, shares[:], ALU.mult, ALU.max)
        nc.vector.tensor_scalar(sign2[:], shares[:, 0, :], 0.0, 2.0, ALU.is_ge, ALU.mult)
        nc.vector.tensor_scalar(floor[:], sizes[:, 1, :], REL_FLOOR, ABS_FLOOR, ALU.mult, ALU.add)
        nc.vector.tensor_copy(factor[split:, :], shares[split:, 1, :])
        nc.vector.tensor_tensor(size[:], floor[:], sizes[:, 0, :], ALU.max)
        nc.vector.scalar_tensor_tensor(lam_safe[:], sign2[:], -1.0, size[:], ALU.add, ALU.mult)
        nc.vector.reciprocal(inverse[:], lam_safe[:])
        nc.vector.tensor_tensor(factor[:split, :], shares[:split, 1, :], inverse[:split, :], ALU.mult)
        nc.sync.dma_start(out[0].rearrange("(p e) -> p e", e=RUN), lam_safe[:])
        nc.sync.dma_start(w2w[:], w2_words[0].rearrange("p c r -> p (c r)").bitcast(I32))
        nc.gpsimd.memset(w2s[:].bitcast(I32), 0)
        for q in range(4):
            nc.sync.dma_start(w2s[32 * q : 32 * q + 4, :].bitcast(I32), w2_scales[0, 4 * q : 4 * q + 4, :].bitcast(I32))
        nc.sync.dma_start(lam_wide[:], lam[:, TURNED * P :])
        with nc.allow_non_contiguous_dma(reason="one share a partition"):
            nc.sync.dma_start(lam_col[:], out[0, : TURNED * P].rearrange("(c p) -> p c", p=P))

        xs = keep.tile([P, S], U8, name="xs", align_bytes=64)
        xw = keep.tile([P, S], U32, name="xw", align_bytes=64)
        nc.vector.tensor_copy(xs[:], xs_all[:].indirect(offs_sb[:]))

        w1_bf = keep.tile([P, PACK, P, PACK], BF16, name="w1_bf", align_bytes=64)
        dst = w1_bf[:].rearrange("p t m j -> p m j t")
        for raw, (c0, n) in zip(w1_raw, W1_PARTS):
            nc.scalar.copy(dst[:, c0 // PACK : (c0 + n) // PACK], raw[:].rearrange("p j (m t) -> p m j t", t=PACK))
        factors = keep.tile([P, S], F32, name="factors", align_bytes=64)
        for e0 in range(0, RUN, PACK):
            spread = quarters(3 + e0 // PACK)
            for i in range(PACK):
                nc.tensor.transpose(spread[:, i, :], factor[:, e0 + i : e0 + i + 1].to_broadcast([P, P]), ident[:])
            nc.scalar.copy(factors[:].rearrange("q (n e) -> q n e", e=RUN)[:, :, e0 : e0 + PACK], spread.rearrange("q e n -> q n e"))
        w1s = keep.tile([P, H], U8, name="w1s", align_bytes=64)
        w1w_first = keep.tile([P, P], U32, name="w1w_first", align_bytes=64)
        nc.vector.quantize_mx(out=w1w_first[:].bitcast(FP8X4), scales=w1s[:, :P], in_=w1_bf[:, 0].rearrange("p m j -> p (m j)"))

        for j0, n in FINE:
            nc.vector.tensor_copy(xw[:, j0 : j0 + n], xw_all[:].bitcast(U32).indirect(entries(offs_sb, j0, n)))

        w1w_rest = keep.tile([P, H - P], U32, name="w1w_rest", tag="xw_all", align_bytes=64)
        nc.vector.quantize_mx(out=w1w_rest[:, :P].bitcast(FP8X4), scales=w1s[:, P : 2 * P], in_=w1_bf[:, 1].rearrange("p m j -> p (m j)"))
        nc.vector.quantize_mx(out=w1w_rest[:, P:].bitcast(FP8X4), scales=w1s[:, 2 * P :], in_=w1_bf[:, 2:].rearrange("p t m j -> p (t m j)"))
        w1w = [w1w_first[:]] + [w1w_rest[:, i * P : (i + 1) * P] for i in range(PACK - 1)]

        h = [keep.tile([P, S], F32, name=f"h{t}", tag=f"h{t}", align_bytes=64) for t in range(PACK)]
        made = 0
        for t in range(PACK):
            cols = slice(t * P, (t + 1) * P)
            for j0, n in FINE if t == 0 else COARSE:
                u = banks[made % 3]
                made += 1
                nc.tensor.matmul_mx(out=u[:, :n], lhsT=w1w[t].bitcast(FP8X4), lhsT_scale=w1s[:, cols],
                                    rhs=xw[:, j0 : j0 + n].bitcast(FP8X4), rhs_scale=xs[:, j0 : j0 + n], start=True, stop=True)
                nc.scalar.activation(h[t][:, j0 : j0 + n], u[:, :n], ACT.Gelu_apprx_tanh)

        partner = {}
        total = [quarters(b) for b in (3, 4, 5, 6, 7, 3)]
        back_bank = (0, 1, 2, 0, 1, 2)
        y_bank = {0: 4, 256: 5, 512: 6, 768: 7, 896: 3}

        def fetch(g, t):
            j0 = g * GROUP
            if t == 0:
                partner[g] = keep.tile([P, PACK, GROUP], F32, name="partner", tag="partner", bufs=2, align_bytes=64)
            nc.vector.tensor_tensor(partner[g][:, t, :], h[t][:].indirect(entries(pos_sb, j0, GROUP)), factors[:, j0 : j0 + GROUP], ALU.mult)

        def add_turned(g, t):
            for lo in range(0, GROUP, P):
                c = (g * GROUP + lo) // P
                nc.tensor.matmul(total[c][:, t, :], h[t][:, c * P : (c + 1) * P], ident[:], start=(t == 0), stop=False, is_transpose=True)
                nc.tensor.matmul(total[c][:, t, :], partner[g][:, t, lo : lo + P], ident[:], start=False, stop=(t == PACK - 1), is_transpose=True)

        def second_layer(j0, n, z_bf, zw, last):
            zs = keep.tile([P, n], U8, name=f"zs{j0}", align_bytes=64)
            nc.vector.quantize_mx(out=zw.bitcast(FP8X4), scales=zs[:], in_=z_bf[:].rearrange("p n t -> p (n t)"))
            y = banks[y_bank[j0]][:, :n]
            nc.tensor.matmul_mx(out=y, lhsT=w2w[:].bitcast(FP8X4), lhsT_scale=w2s[:],
                                rhs=zw.bitcast(FP8X4), rhs_scale=zs[:], start=True, stop=True)
            y_sb = keep.tile([P, n], F32, name=f"y_sb{j0}", align_bytes=64)
            if last:
                nc.vector.tensor_copy(y_sb[:], y)
            else:
                nc.scalar.copy(y_sb[:], y)
            nc.sync.dma_start(out[:, j0 : j0 + n], y_sb[:])

        def finish_turned(g):
            j0 = g * GROUP
            z_bf = keep.tile([P, GROUP, PACK], BF16, name=f"z_bf{j0}", tag=f"z_bf{j0}", align_bytes=64)
            for lo in range(0, GROUP, P):
                c = (j0 + lo) // P
                z_t = keep.tile([P, 2, P, 2], BF16, name=f"z_t{c}", tag=f"z_t{c}", align_bytes=64)
                nc.scalar.activation(z_t[:], total[c].rearrange("j (u e) p -> j u p e", e=2), ACT.Copy, scale=lam_col[:, c : c + 1])
                pairs = z_t[:].rearrange("j u p e -> j (u p e)").bitcast(F32)
                back = quarters(back_bank[c])[:, :2, :]
                for u in range(2):
                    nc.tensor.transpose(back[:, u, :], pairs[:, u * P : (u + 1) * P], ident[:])
                woven = z_bf[:, lo : lo + P, :].rearrange("p j t -> p (j t)").bitcast(F32).rearrange("p (j u) -> p j u", u=2)
                nc.scalar.copy(woven, back.rearrange("p u j -> p j u"))
            return z_bf

        for t in range(PACK):
            for g in range(2):
                fetch(g, t)
                add_turned(g, t)
        turned = [finish_turned(0)]
        for t in range(PACK):
            fetch(2, t)
            add_turned(2, t)
        turned.append(finish_turned(1))
        j0 = TURNED * P
        own = keep.tile([P, PACK, GROUP], F32, name="own", tag="z_t0", align_bytes=64)
        for t in range(PACK):
            nc.vector.tensor_tensor(own[:, t, :], h[t][:, j0:], lam_wide[:], ALU.mult)
        turned.append(finish_turned(2))
        for t in range(PACK):
            fetch(3, t)
        for g, tag in enumerate(("h2", "h3", "zw2")):
            zw = keep.tile([P, GROUP], U32, name=f"zw{g}", tag=tag, align_bytes=64)
            second_layer(g * GROUP, GROUP, turned[g], zw[:], False)
        zw_last = keep.tile([P, GROUP], U32, name="zw_last", tag="z_bf512", align_bytes=64)
        for lo in range(0, GROUP, P):
            z_bf = keep.tile([P, P, PACK], BF16, name=f"z_bf{j0 + lo}", align_bytes=64)
            nc.vector.tensor_tensor(
                z_bf[:].rearrange("p (c i) t -> p c t i", i=4),
                own[:, :, lo : lo + P].rearrange("p t (c i) -> p c t i", i=4),
                partner[3][:, :, lo : lo + P].rearrange("p t (c i) -> p c t i", i=4),
                ALU.add,
            )
            second_layer(j0 + lo, P, z_bf, zw_last[:, lo : lo + P], lo + P == GROUP)
